import numpy as np, ml_dtypes
CORES = [23,39,55,63,87,103,111,127,18,34,50,58,82,98,106,122]
N = 16
import mx_ref
NC, KT = 128, 4
FROM = [14,5,3,15,12,13,2,8,9,0,1,7,10,11,6,4]
BF = ml_dtypes.bfloat16
def setup_inputs(rng):
    def f(*shape):
        return mx_ref.flush((rng.standard_normal(shape, dtype=np.float32) * np.exp2(rng.integers(-2, 3, shape[:-1] + (1,)))).astype(BF))
    return {"w": f(N, 128, KT * 512), "x": f(N, 128, KT * 4 * NC)}
def setup_inputs_blocks(rng):
    d = setup_inputs(rng)
    for k in ("w", "x"): d[k] = mx_ref.spread(d[k], rng, 1)
    return d
def setup_inputs_wide(rng):
    d = setup_inputs(rng)
    for k in ("w", "x"): d[k] = mx_ref.flush((d[k].astype(np.float32) * np.exp2(rng.integers(-8, 9, (N, 1, 1))).astype(np.float32)).astype(BF))
    return d
def setup_inputs_zeros(rng):
    d = setup_inputs(rng); v = d["x"].reshape(N, 128, -1, 4).copy()
    v[np.broadcast_to((rng.random((N, 1, v.shape[2], 1)) < 0.33), v.shape)] = 0
    d["x"] = v.reshape(d["x"].shape)
    return d
def reference(w, x):
    y = np.zeros((N, 128, NC), np.float32)
    for r in range(N):
        for t in range(KT):
            p = mx_ref.matmul(mx_ref.quantize(w[r][:, 512 * t:512 * t + 512]), mx_ref.quantize(x[FROM[r]][:, 4 * NC * t:4 * NC * t + 4 * NC]))
            y[r] = p if t == 0 else y[r] + p
    return {"y": y}

@@ -1,0 +1,70 @@
+from concourse.mybir import dt
+
+NT = 4
+WC = 128
+EC = 4 * WC
+NENG = 8
+
+SCRATCH = {
+    "xb": ("sbuf", [128, NT * EC], "bfloat16"),
+    "wb": ("sbuf", [128, NT * EC], "bfloat16"),
+    "xq": ("sbuf", [128, NT * WC], "float8_e4m3fn_x4"),
+    "xs": ("sbuf", [128, NT * WC], "uint8"),
+    "wq": ("sbuf", [128, NT * WC], "float8_e4m3fn_x4"),
+    "ws": ("sbuf", [128, NT * WC], "uint8"),
+    "rq": ("sbuf", [128, NT * WC], "float8_e4m3fn_x4"),
+    "rs": ("sbuf", [128, NT * WC], "uint8"),
+    "acc": ("psum", [128, 512], "float32"),
+    "yb": ("sbuf", [128, WC], "float32"),
+}
+SEMAPHORES = ["lx0", "lxr", "lw", "qx0", "qxr", "qw", "head", "rest", "sent", "mm", "cp", "st"]
+
+
+def _engines(mask, k):
+    bits = [b for b in range(mask.bit_length()) if (mask >> b) & 1][:k]
+    return sum(1 << b for b in bits)
+
+
+def rank_program(g, core, T, topo):
+    rank = T.rank_of(core)
+    if rank is None:
+        return
+    frm = T.tables["FROM"]
+    dst = T.cores[frm.index(rank)]
+    rid, pid, _ = topo.addr(dst)
+    eng = _engines(topo.mask(core, dst), NENG)
+    S = T.sem
+
+    g.sync.dma_start(T.xb[:, 0:EC], T.x[:, 0:EC]).then_inc(S.lx0, 16)
+    g.sync.dma_start(T.xb[:, EC:NT * EC], T.x[:, EC:NT * EC]).then_inc(S.lxr, 16)
+    g.sync.dma_start(T.wb[:], T.w[:]).then_inc(S.lw, 16)
+
+    g.vector.wait_ge(S.lx0, 16)
+    g.vector.quantize_mx(T.xq[:, 0:WC], T.xs[:, 0:WC], T.xb[:, 0:EC]).then_inc(S.qx0, 1)
+    g.vector.wait_ge(S.lxr, 16)
+    g.vector.quantize_mx(T.xq[:, WC:NT * WC], T.xs[:, WC:NT * WC], T.xb[:, EC:NT * EC]).then_inc(S.qxr, 1)
+    g.vector.wait_ge(S.lw, 16)
+    g.vector.quantize_mx(T.wq[:], T.ws[:], T.wb[:]).then_inc(S.qw, 1)
+
+    g.wait_ge(S.qx0, 1)
+    g.remote_dma(T.rq[:, 0:WC].bitcast(dt.uint8), T.xq[:, 0:WC].bitcast(dt.uint8), S.head, S.sent, pid, rid, eng)
+    g.wait_ge(S.qxr, 1)
+    g.remote_dma(T.rs[:], T.xs[:], S.head, S.sent, pid, rid, eng)
+    g.remote_dma(T.rq[:, WC:NT * WC].bitcast(dt.uint8), T.xq[:, WC:NT * WC].bitcast(dt.uint8),
+                 S.rest, S.sent, pid, rid, eng)
+
+    g.tensor.wait_ge(S.qw, 1)
+    g.tensor.wait_ge(S.head, 2 * NENG)
+    for t in range(NT):
+        if t == 1:
+            g.tensor.wait_ge(S.rest, NENG)
+        c = slice(t * WC, (t + 1) * WC)
+        mmi = g.tensor.matmul_mx(T.acc[:, 0:WC], T.wq[:, c], T.ws[:, c], T.rq[:, c], T.rs[:, c], t == 0, t == NT - 1)
+    mmi.then_inc(S.mm, 1)
+
+    g.vector.wait_ge(S.mm, 1)
+    g.vector.tensor_copy(T.yb[:], T.acc[:, 0:WC]).then_inc(S.cp, 1)
+    g.sync.wait_ge(S.cp, 1)
+    g.sync.dma_start(T.y[:], T.yb[:]).then_inc(S.st, 16)
+    g.sync.wait_ge(S.st, 16)
+    g.wait_ge(S.sent, 3 * NENG)

@@ -1,9 +1,16 @@
+from concourse.bass import DstId, RemoteDMATransfer
 from concourse.mybir import dt
 
 NT = 4
 WC = 128
 EC = 4 * WC
 NENG = 8
+
+PIECES = {"0": ("q", 0, WC), "1": ("q", WC, 2 * WC), "2": ("q", 2 * WC, 3 * WC),
+          "B": ("s", 0, NT * WC), "3": ("q", 3 * WC, NT * WC)}
+ORDER = ["0", "1", "2", "B", "3"]
+EARLY = ["0", "1", "2"]
+NEEDS = {"0": 0, "1": 1, "2": 2, "B": 3, "3": 3}
 
 SCRATCH = {
     "xb": ("sbuf", [128, NT * EC], "bfloat16"),
@@ -14,52 +21,153 @@ SCRATCH = {
     "ws": ("sbuf", [128, NT * WC], "uint8"),
     "rq": ("sbuf", [128, NT * WC], "float8_e4m3fn_x4"),
     "rs": ("sbuf", [128, NT * WC], "uint8"),
+    "fq": ("sbuf", [128, NT * WC], "float8_e4m3fn_x4"),
     "acc": ("psum", [128, 512], "float32"),
     "yb": ("sbuf", [128, WC], "float32"),
 }
-SEMAPHORES = ["lx0", "lxr", "lw", "qx0", "qxr", "qw", "head", "rest", "sent", "mm", "cp", "st"]
+SEMAPHORES = (["lx%d" % t for t in range(NT)] + ["qx%d" % t for t in range(NT)]
+              + ["lw%d" % t for t in range(NT)] + ["qw%d" % t for t in range(NT)]
+              + ["r" + p for p in ORDER] + ["f" + p for p in EARLY] + ["sent", "mm", "cp", "st"])
 
 
-def _engines(mask, k):
-    bits = [b for b in range(mask.bit_length()) if (mask >> b) & 1][:k]
+def _count(mask):
+    return sum((mask >> b) & 1 for b in range(mask.bit_length()))
+
+
+def _engines(mask, k, skip=0):
+    bits = [b for b in range(mask.bit_length()) if (mask >> b) & 1][skip:skip + k]
     return sum(1 << b for b in bits)
 
 
+def _links(topo, src, dst):
+    a, b, d = topo.chip(src), topo.chip(dst), topo.die(src)
+    out = []
+    if a == b:
+        return out
+    if not topo.same_plane(a, b):
+        m = [k for k in range(topo.CHIPS) if topo.mates(a, k)][0]
+        out.append(("mate", a, m, d))
+        a = m
+    if a != b:
+        out += [("out", a, d), ("in", b, d)]
+    return out
+
+
+def _plan(T, topo):
+    cores, frm = T.cores, T.tables["FROM"]
+    flow = {cores[frm[r]]: cores[r] for r in range(len(cores))}
+
+    def neighbour(c):
+        nb = [k for k in cores if topo.chip(k) == topo.chip(c) and topo.die(k) != topo.die(c)]
+        return nb[0] if nb else None
+
+    def loads(via):
+        ld = {}
+        for s, d in flow.items():
+            for l in _links(topo, via.get(s, s), d):
+                ld[l] = ld.get(l, 0) + 1
+        return ld
+
+    cand = []
+    for s, d in flow.items():
+        nb = neighbour(s)
+        if (topo.chip(s) != topo.chip(d) and nb is not None and topo.chip(flow[nb]) == topo.chip(nb)
+                and topo.may_write(nb, d)):
+            cand.append(s)
+    best = None
+    for bits in range(1 << len(cand)):
+        via = {s: neighbour(s) for i, s in enumerate(cand) if (bits >> i) & 1}
+        ld = loads(via).values()
+        key = (max(ld), sum(v * v for v in ld), len(via))
+        if best is None or key < best[0]:
+            best = (key, via)
+    turned = best[1]
+    ld = loads(turned)
+    part = {}
+    for s, d in flow.items():
+        nb = neighbour(s)
+        if (s not in turned and nb is not None and nb not in turned.values() and topo.may_write(nb, d)
+                and any(ld[l] > 1 for l in _links(topo, s, d))):
+            part[s] = nb
+
+    first, second = [], []
+    for s, d in flow.items():
+        if s in turned.values():
+            own = _engines(topo.mask(s, d), NENG)
+            first.append((s, d, ORDER[0], "x", "r", own, False))
+            each = NENG // (len(ORDER) - 1)
+            for i, p in enumerate(ORDER[1:]):
+                first.append((s, d, p, "x", "r", _engines(own, each, i * each), True))
+            continue
+        for p in ORDER:
+            if (s in turned and p in EARLY) or (s in part and p == ORDER[0]):
+                nb = turned.get(s, part.get(s))
+                first.append((s, nb, p, "x", "f", _engines(topo.mask(s, nb), NENG), False))
+                second.append((nb, d, p, "f", "r", _engines(topo.mask(nb, d), NENG), False))
+            else:
+                first.append((s, d, p, "x", "r", _engines(topo.mask(s, d), NENG), False))
+    order = {flow[s]: [1, 2, 3, 0] for s in part}
+    order.update({flow[s]: [0, 1, 3, 2] for s in turned})
+    return first + second, order
+
+
 def rank_program(g, core, T, topo):
-    rank = T.rank_of(core)
-    if rank is None:
+    if T.rank_of(core) is None:
         return
-    frm = T.tables["FROM"]
-    dst = T.cores[frm.index(rank)]
-    rid, pid, _ = topo.addr(dst)
-    eng = _engines(topo.mask(core, dst), NENG)
     S = T.sem
+    writes, order = _plan(T, topo)
 
-    g.sync.dma_start(T.xb[:, 0:EC], T.x[:, 0:EC]).then_inc(S.lx0, 16)
-    g.sync.dma_start(T.xb[:, EC:NT * EC], T.x[:, EC:NT * EC]).then_inc(S.lxr, 16)
-    g.sync.dma_start(T.wb[:], T.w[:]).then_inc(S.lw, 16)
+    def view(buf, p):
+        kind, lo, hi = PIECES[p]
+        v = T[buf + kind][:, lo:hi]
+        return v.bitcast(dt.uint8) if kind == "q" else v
 
-    g.vector.wait_ge(S.lx0, 16)
-    g.vector.quantize_mx(T.xq[:, 0:WC], T.xs[:, 0:WC], T.xb[:, 0:EC]).then_inc(S.qx0, 1)
-    g.vector.wait_ge(S.lxr, 16)
-    g.vector.quantize_mx(T.xq[:, WC:NT * WC], T.xs[:, WC:NT * WC], T.xb[:, EC:NT * EC]).then_inc(S.qxr, 1)
-    g.vector.wait_ge(S.lw, 16)
-    g.vector.quantize_mx(T.wq[:], T.ws[:], T.wb[:]).then_inc(S.qw, 1)
+    def due(to, p):
+        return sum(_count(w[5]) for w in writes if w[1] == core and w[2] == p and w[4] == to)
 
-    g.wait_ge(S.qx0, 1)
-    g.remote_dma(T.rq[:, 0:WC].bitcast(dt.uint8), T.xq[:, 0:WC].bitcast(dt.uint8), S.head, S.sent, pid, rid, eng)
-    g.wait_ge(S.qxr, 1)
-    g.remote_dma(T.rs[:], T.xs[:], S.head, S.sent, pid, rid, eng)
-    g.remote_dma(T.rq[:, WC:NT * WC].bitcast(dt.uint8), T.xq[:, WC:NT * WC].bitcast(dt.uint8),
-                 S.rest, S.sent, pid, rid, eng)
-
-    g.tensor.wait_ge(S.qw, 1)
-    g.tensor.wait_ge(S.head, 2 * NENG)
     for t in range(NT):
-        if t == 1:
-            g.tensor.wait_ge(S.rest, NENG)
+        g.sync.dma_start(T.xb[:, t * EC:(t + 1) * EC], T.x[:, t * EC:(t + 1) * EC]).then_inc(S["lx%d" % t], 16)
+    for t in range(NT):
+        g.sync.dma_start(T.wb[:, t * EC:(t + 1) * EC], T.w[:, t * EC:(t + 1) * EC]).then_inc(S["lw%d" % t], 16)
+
+    for t in range(NT):
+        g.vector.wait_ge(S["lx%d" % t], 16)
+        g.vector.quantize_mx(T.xq[:, t * WC:(t + 1) * WC], T.xs[:, t * WC:(t + 1) * WC],
+                             T.xb[:, t * EC:(t + 1) * EC]).then_inc(S["qx%d" % t], 1)
+    for t in range(NT):
+        g.vector.wait_ge(S["lw%d" % t], 16)
+        g.vector.quantize_mx(T.wq[:, t * WC:(t + 1) * WC], T.ws[:, t * WC:(t + 1) * WC],
+                             T.wb[:, t * EC:(t + 1) * EC]).then_inc(S["qw%d" % t], 1)
+
+    mine = [w for w in writes if w[0] == core]
+    left = sum(_count(w[5]) for w in mine)
+    packed = -1
+    pack = []
+    for n, (s, d, p, frm_buf, to_buf, m, fused) in enumerate(mine):
+        rid, pid, _ = topo.addr(d)
+        if frm_buf == "x":
+            need = max(NEEDS[w[2]] for w in mine[n:] if w[6]) if fused else NEEDS[p]
+            while packed < need:
+                packed += 1
+                g.wait_ge(S["qx%d" % packed], 1)
+        else:
+            g.wait_ge(S["f" + p], due("f", p))
+        if not fused:
+            g.remote_dma(view(to_buf, p), view(frm_buf, p), S[to_buf + p], S.sent, pid, rid, m)
+            continue
+        pack.append(RemoteDMATransfer(dst_ids=[DstId(rid=rid, pnc=pid)], dma_engine_mask=m,
+                                      remote_sem=S[to_buf + p], src=view(frm_buf, p), dst=view(to_buf, p)))
+        if n + 1 == len(mine) or not mine[n + 1][6]:
+            g.remote_dma_fused(pack, local_sem=S.sent)
+            pack = []
+
+    g.tensor.wait_ge(S.rB, due("r", "B"))
+    for i, t in enumerate(order.get(core, [0, 1, 2, 3])):
+        g.tensor.wait_ge(S["qw%d" % t], 1)
+        g.tensor.wait_ge(S["r%d" % t], due("r", "%d" % t))
         c = slice(t * WC, (t + 1) * WC)
-        mmi = g.tensor.matmul_mx(T.acc[:, 0:WC], T.wq[:, c], T.ws[:, c], T.rq[:, c], T.rs[:, c], t == 0, t == NT - 1)
+        mmi = g.tensor.matmul_mx(T.acc[:, 0:WC], T.wq[:, c], T.ws[:, c], T.rq[:, c], T.rs[:, c],
+                                 i == 0, i == NT - 1)
     mmi.then_inc(S.mm, 1)
 
     g.vector.wait_ge(S.mm, 1)
@@ -67,4 +175,4 @@ def rank_program(g, core, T, topo):
     g.sync.wait_ge(S.cp, 1)
     g.sync.dma_start(T.y[:], T.yb[:]).then_inc(S.st, 16)
     g.sync.wait_ge(S.st, 16)
-    g.wait_ge(S.sent, 3 * NENG)
+    g.wait_ge(S.sent, left)

from concourse.bass import DstId, RemoteDMATransfer
from concourse.mybir import dt

NT = 4
WC = 128
EC = 4 * WC
NENG = 8

PIECES = {"0": ("q", 0, WC), "1": ("q", WC, 2 * WC), "2": ("q", 2 * WC, 3 * WC),
          "B": ("s", 0, NT * WC), "3": ("q", 3 * WC, NT * WC)}
ORDER = ["0", "1", "2", "B", "3"]
EARLY = ["0", "1", "2"]
NEEDS = {"0": 0, "1": 1, "2": 2, "B": 3, "3": 3}

SCRATCH = {
    "xb": ("sbuf", [128, NT * EC], "bfloat16"),
    "wb": ("sbuf", [128, NT * EC], "bfloat16"),
    "xq": ("sbuf", [128, NT * WC], "float8_e4m3fn_x4"),
    "xs": ("sbuf", [128, NT * WC], "uint8"),
    "wq": ("sbuf", [128, NT * WC], "float8_e4m3fn_x4"),
    "ws": ("sbuf", [128, NT * WC], "uint8"),
    "rq": ("sbuf", [128, NT * WC], "float8_e4m3fn_x4"),
    "rs": ("sbuf", [128, NT * WC], "uint8"),
    "fq": ("sbuf", [128, NT * WC], "float8_e4m3fn_x4"),
    "acc": ("psum", [128, 512], "float32"),
    "yb": ("sbuf", [128, WC], "float32"),
}
SEMAPHORES = (["lx%d" % t for t in range(NT)] + ["qx%d" % t for t in range(NT)]
              + ["lw%d" % t for t in range(NT)] + ["qw%d" % t for t in range(NT)]
              + ["r" + p for p in ORDER] + ["f" + p for p in EARLY] + ["sent", "mm", "cp", "st"])


def _count(mask):
    return sum((mask >> b) & 1 for b in range(mask.bit_length()))


def _engines(mask, k, skip=0):
    bits = [b for b in range(mask.bit_length()) if (mask >> b) & 1][skip:skip + k]
    return sum(1 << b for b in bits)


def _links(topo, src, dst):
    a, b, d = topo.chip(src), topo.chip(dst), topo.die(src)
    out = []
    if a == b:
        return out
    if not topo.same_plane(a, b):
        m = [k for k in range(topo.CHIPS) if topo.mates(a, k)][0]
        out.append(("mate", a, m, d))
        a = m
    if a != b:
        out += [("out", a, d), ("in", b, d)]
    return out


def _plan(T, topo):
    cores, frm = T.cores, T.tables["FROM"]
    flow = {cores[frm[r]]: cores[r] for r in range(len(cores))}

    def neighbour(c):
        nb = [k for k in cores if topo.chip(k) == topo.chip(c) and topo.die(k) != topo.die(c)]
        return nb[0] if nb else None

    def loads(via):
        ld = {}
        for s, d in flow.items():
            for l in _links(topo, via.get(s, s), d):
                ld[l] = ld.get(l, 0) + 1
        return ld

    cand = []
    for s, d in flow.items():
        nb = neighbour(s)
        if (topo.chip(s) != topo.chip(d) and nb is not None and topo.chip(flow[nb]) == topo.chip(nb)
                and topo.may_write(nb, d)):
            cand.append(s)
    best = None
    for bits in range(1 << len(cand)):
        via = {s: neighbour(s) for i, s in enumerate(cand) if (bits >> i) & 1}
        ld = loads(via).values()
        key = (max(ld), sum(v * v for v in ld), len(via))
        if best is None or key < best[0]:
            best = (key, via)
    turned = best[1]
    ld = loads(turned)
    part = {}
    for s, d in flow.items():
        nb = neighbour(s)
        if (s not in turned and nb is not None and nb not in turned.values() and topo.may_write(nb, d)
                and any(ld[l] > 1 for l in _links(topo, s, d))):
            part[s] = nb

    first, second = [], []
    for s, d in flow.items():
        if s in turned.values():
            own = _engines(topo.mask(s, d), NENG)
            first.append((s, d, ORDER[0], "x", "r", own, False))
            each = NENG // (len(ORDER) - 1)
            for i, p in enumerate(ORDER[1:]):
                first.append((s, d, p, "x", "r", _engines(own, each, i * each), True))
            continue
        for p in ORDER:
            if (s in turned and p in EARLY) or (s in part and p == ORDER[0]):
                nb = turned.get(s, part.get(s))
                first.append((s, nb, p, "x", "f", _engines(topo.mask(s, nb), NENG), False))
                second.append((nb, d, p, "f", "r", _engines(topo.mask(nb, d), NENG), False))
            else:
                first.append((s, d, p, "x", "r", _engines(topo.mask(s, d), NENG), False))
    order = {flow[s]: [1, 2, 3, 0] for s in part}
    order.update({flow[s]: [0, 1, 3, 2] for s in turned})
    return first + second, order


def rank_program(g, core, T, topo):
    if T.rank_of(core) is None:
        return
    S = T.sem
    writes, order = _plan(T, topo)

    def view(buf, p):
        kind, lo, hi = PIECES[p]
        v = T[buf + kind][:, lo:hi]
        return v.bitcast(dt.uint8) if kind == "q" else v

    def due(to, p):
        return sum(_count(w[5]) for w in writes if w[1] == core and w[2] == p and w[4] == to)

    for t in range(NT):
        g.sync.dma_start(T.xb[:, t * EC:(t + 1) * EC], T.x[:, t * EC:(t + 1) * EC]).then_inc(S["lx%d" % t], 16)
    for t in range(NT):
        g.sync.dma_start(T.wb[:, t * EC:(t + 1) * EC], T.w[:, t * EC:(t + 1) * EC]).then_inc(S["lw%d" % t], 16)

    for t in range(NT):
        g.vector.wait_ge(S["lx%d" % t], 16)
        g.vector.quantize_mx(T.xq[:, t * WC:(t + 1) * WC], T.xs[:, t * WC:(t + 1) * WC],
                             T.xb[:, t * EC:(t + 1) * EC]).then_inc(S["qx%d" % t], 1)
    for t in range(NT):
        g.vector.wait_ge(S["lw%d" % t], 16)
        g.vector.quantize_mx(T.wq[:, t * WC:(t + 1) * WC], T.ws[:, t * WC:(t + 1) * WC],
                             T.wb[:, t * EC:(t + 1) * EC]).then_inc(S["qw%d" % t], 1)

    mine = [w for w in writes if w[0] == core]
    left = sum(_count(w[5]) for w in mine)
    packed = -1
    pack = []
    for n, (s, d, p, frm_buf, to_buf, m, fused) in enumerate(mine):
        rid, pid, _ = topo.addr(d)
        if frm_buf == "x":
            need = max(NEEDS[w[2]] for w in mine[n:] if w[6]) if fused else NEEDS[p]
            while packed < need:
                packed += 1
                g.wait_ge(S["qx%d" % packed], 1)
        else:
            g.wait_ge(S["f" + p], due("f", p))
        if not fused:
            g.remote_dma(view(to_buf, p), view(frm_buf, p), S[to_buf + p], S.sent, pid, rid, m)
            continue
        pack.append(RemoteDMATransfer(dst_ids=[DstId(rid=rid, pnc=pid)], dma_engine_mask=m,
                                      remote_sem=S[to_buf + p], src=view(frm_buf, p), dst=view(to_buf, p)))
        if n + 1 == len(mine) or not mine[n + 1][6]:
            g.remote_dma_fused(pack, local_sem=S.sent)
            pack = []

    g.tensor.wait_ge(S.rB, due("r", "B"))
    for i, t in enumerate(order.get(core, [0, 1, 2, 3])):
        g.tensor.wait_ge(S["qw%d" % t], 1)
        g.tensor.wait_ge(S["r%d" % t], due("r", "%d" % t))
        c = slice(t * WC, (t + 1) * WC)
        mmi = g.tensor.matmul_mx(T.acc[:, 0:WC], T.wq[:, c], T.ws[:, c], T.rq[:, c], T.rs[:, c],
                                 i == 0, i == NT - 1)
    mmi.then_inc(S.mm, 1)

    g.vector.wait_ge(S.mm, 1)
    g.vector.tensor_copy(T.yb[:], T.acc[:, 0:WC]).then_inc(S.cp, 1)
    g.sync.wait_ge(S.cp, 1)
    g.sync.dma_start(T.y[:], T.yb[:]).then_inc(S.st, 16)
    g.sync.wait_ge(S.st, 16)
    g.wait_ge(S.sent, left)
